import numpy as np
import ml_dtypes


def mxq(x, axis, fmt="e4m3"):
    dtype, down = {"e4m3": (ml_dtypes.float8_e4m3fn, 7), "e5m2": (ml_dtypes.float8_e5m2, 14)}[fmt]
    v = np.moveaxis(np.asarray(x, np.float32).astype(ml_dtypes.bfloat16).astype(np.float64), axis, -1)
    blocks = v.reshape(v.shape[:-1] + (-1, 32))
    amax = np.abs(blocks).max(-1, keepdims=True)
    byte = np.maximum(np.where(amax > 0, np.frexp(amax)[1] - 1 + 127, 0) - down, 1)
    scale = np.exp2(byte - 127.0)
    codes = (blocks / scale).astype(np.float32).astype(dtype).astype(np.float64)
    return np.moveaxis((codes * scale).reshape(v.shape), -1, axis)


WIDE = False


def mx_kscale(k):
    if not WIDE:
        return np.ones(k)
    levels = np.array([10, -10, 5, -5, 0])
    if k % 512:
        return np.exp2(np.random.permutation(np.resize(levels, k // 32))).repeat(32)
    a = np.empty((k // 512, 16))
    for p in range(k // 512):
        a[p, :8] = np.random.permutation(np.resize(levels, 8))
        for g in range(8):
            far = levels[np.abs(levels - a[p, g]) >= 10]
            a[p, g + 8] = far[np.random.randint(len(far))]
    return np.exp2(a.ravel()).repeat(32)


def f64(x):
    return np.asarray(x).astype(np.float64)


def striped(idx):
    return np.tile(np.asarray(idx).reshape(-1, 16).T, (8, 1)).astype(np.uint16)


def unstriped(offs):
    return offs[:16].T.reshape(-1).astype(np.int64)


E2M1 = np.array([0.0, 0.5, 1.0, 1.5, 2.0, 3.0, 4.0, 6.0, -0.0, -0.5, -1.0, -1.5, -2.0, -3.0, -4.0, -6.0])


def pack_weight(w, fmt):
    k, n = w.shape
    w = f64(np.asarray(w, np.float32).astype(ml_dtypes.bfloat16)).reshape(k // 32, 32, n)
    amax = np.abs(w).max(1)
    if fmt == "e4m3":
        byte = np.frexp(amax)[1] - 1 + 127 - 7
    else:
        mant, ex = np.frexp(amax / 6.0)
        byte = np.where(mant > 0.5, ex, ex - 1) + 127
    byte = np.clip(np.where(amax > 0, byte, 1), 1, 254)
    scaled = (w * np.exp2(127.0 - byte)[:, None, :]).reshape(k, n).astype(np.float32)
    by_word = np.ascontiguousarray(scaled.reshape(k // 512, 128, 4, n).transpose(0, 1, 3, 2))
    if fmt == "e4m3":
        words = by_word.astype(ml_dtypes.float8_e4m3fn).view(np.uint8)
    else:
        c = by_word.astype(ml_dtypes.float4_e2m1fn).view(np.uint8) & 0xF
        words = (c[..., 0::2] | (c[..., 1::2] << 4)).reshape(k // 512, 128, 2 * n)
    return np.ascontiguousarray(words), np.ascontiguousarray(byte.astype(np.uint8).reshape(k // 512, 16, n))


def unpack_weight(words, scales, fmt):
    g, _, n = scales.shape
    words = np.ascontiguousarray(words).reshape(g, 128, n, -1)
    if fmt == "e4m3":
        vals = words.view(ml_dtypes.float8_e4m3fn).astype(np.float64)
    else:
        nib = np.empty((g, 128, n, 4), np.uint8)
        nib[..., 0::2] = words & 0xF
        nib[..., 1::2] = words >> 4
        vals = E2M1[nib]
    vals = vals * np.repeat(np.exp2(scales.astype(np.float64) - 127.0), 8, axis=1)[..., None]
    return vals.transpose(0, 1, 3, 2).reshape(g * 512, n)


D, K, T, U, I, E = 512, 512, 2048, 1024, 512, 256


def setup_inputs():
    n = np.random.standard_normal
    idx = np.random.permutation(T)[:I]
    idx2 = np.random.permutation(U)[:I]
    idx3 = np.random.permutation(U)[:I]
    fd = mx_kscale(D)
    fk = mx_kscale(K)
    pagesp = pack_weight(n((D, T)) / fd[:, None], "e2m1")
    wap = pack_weight(n((D, K)) * 1.0 / np.sqrt(D) * fd[:, None], "e4m3")
    notesp = pack_weight(n((D, U)) / fd[:, None], "e4m3")
    wbp = pack_weight(n((D, K)) * 1.0 / np.sqrt(D) * fd[:, None], "e2m1")
    wop = pack_weight(n((K, E)) * 1.0 / np.sqrt(K) / fk[:, None], "e4m3")
    return {
        "pages_words": pagesp[0],
        "pages_scales": pagesp[1],
        "wa_words": wap[0],
        "wa_scales": wap[1],
        "notes_words": notesp[0],
        "notes_scales": notesp[1],
        "wb_words": wbp[0],
        "wb_scales": wbp[1],
        "kf": (np.random.uniform(0.5, 2.0, (K, 1)) * fk[:, None]).astype(np.float32),
        "wo_words": wop[0],
        "wo_scales": wop[1],
        "offs": striped(idx),
        "offs2": striped(idx2),
        "offs3": striped(idx3),
    }


def reference(pages_words, pages_scales, wa_words, wa_scales, notes_words, notes_scales, wb_words, wb_scales, kf, wo_words, wo_scales, offs, offs2, offs3):
    idx = unstriped(offs)
    idx2 = unstriped(offs2)
    idx3 = unstriped(offs3)
    pagesu = unpack_weight(pages_words, pages_scales, "e2m1")
    wau = unpack_weight(wa_words, wa_scales, "e4m3")
    notesu = unpack_weight(notes_words, notes_scales, "e4m3")
    wbu = unpack_weight(wb_words, wb_scales, "e2m1")
    wou = unpack_weight(wo_words, wo_scales, "e4m3")
    pagesidxg = pagesu[:, idx]
    z = wau.T @ pagesidxg
    h1 = wbu.T @ notesu
    f1 = np.zeros((K, U))
    f1[:, idx2] = z
    c1 = h1 + f1
    w = c1[:, idx3] * f64(kf)
    wq = mxq(w, 0, "e4m3")
    y = wou.T @ wq
    return y

@@ -1,0 +1,226 @@
+from contextlib import ExitStack
+
+import concourse.mybir as mybir
+
+D, K, T, U, I, E = 512, 512, 2048, 1024, 512, 256
+FLOPS = 2 * (D * K * I + D * K * U + K * E * I)
+
+F32 = mybir.dt.float32
+BF16 = mybir.dt.bfloat16
+I32 = mybir.dt.int32
+U32 = mybir.dt.uint32
+U16 = mybir.dt.uint16
+U8 = mybir.dt.uint8
+FP8X4 = mybir.dt.float8_e4m3fn_x4
+FP4X4 = mybir.dt.float4_e2m1fn_x4
+COPY = mybir.ActivationFunctionType.Copy
+ADD = mybir.AluOpType.add
+MULT = mybir.AluOpType.mult
+
+P = 128
+PACK = 4
+BANK = 512
+HALF = I // 2
+LIST_COLS = I // 16
+
+
+def load_scale_rows(nc, plane, rows):
+    for q in range(4):
+        nc.sync.dma_start(plane[32 * q : 32 * q + 4, :].bitcast(I32), rows[4 * q : 4 * q + 4, :].bitcast(I32))
+
+
+def deal(nc, dealt, raw):
+    nc.vector.tensor_copy(dealt.rearrange("p (j m) -> p j m", j=PACK), raw.rearrange("p (m j) -> p j m", j=PACK))
+
+
+def tile_attend_pagesintonotes_kernel(
+    tc, pages_words, pages_scales, wa_words, wa_scales, notes_words, notes_scales, wb_words, wb_scales, kf, wo_words, wo_scales, offs, offs2, offs3, out
+):
+    nc = tc.nc
+    with ExitStack() as ctx:
+        sb = ctx.enter_context(tc.tile_pool(name="sb", bufs=1))
+        psum = ctx.enter_context(tc.psum_pool(name="psum", bufs=1))
+
+        def tile(shape, dtype, name, tag=None):
+            return sb.tile(shape, dtype, name=name, tag=tag or name, align_bytes=64)
+
+        def bank(b, name):
+            return psum.tile([P, BANK], F32, name=name, tag="bank%d" % b)
+
+        def half_of(lst, h):
+            return lst[:, h * LIST_COLS // 2 : (h + 1) * LIST_COLS // 2]
+
+        idx = tile([P, LIST_COLS], U16, "idx")
+        idx2 = tile([P, LIST_COLS], U16, "idx2")
+        idx3 = tile([P, LIST_COLS], U16, "idx3")
+        page_words = tile([P, T], U16, "page_words")
+        page_scales = tile([P, T], U8, "page_scales")
+        wa_raw = tile([P, K], U32, "wa_raw")
+        wa_raw_scales = tile([P, K], U8, "wa_raw_scales")
+        wb_raw_scales = tile([P, K], U8, "wb_raw_scales")
+        f1 = [tile([P, U], F32, "f1_%d" % j) for j in range(2)]
+
+        nc.vector.memset(page_scales[:].bitcast(I32), 0)
+        nc.vector.memset(wa_raw_scales[:].bitcast(I32), 0)
+
+        nc.sync.dma_start(idx[:], offs)
+        nc.sync.dma_start(page_words[:].bitcast(I32), pages_words[0].bitcast(I32))
+        nc.sync.dma_start(wa_raw[:].bitcast(I32), wa_words[0].rearrange("p n t -> p (n t)").bitcast(I32))
+        load_scale_rows(nc, page_scales[:], pages_scales[0])
+        load_scale_rows(nc, wa_raw_scales[:], wa_scales[0])
+        nc.sync.dma_start(idx2[:], offs2)
+        nc.sync.dma_start(idx3[:], offs3)
+
+        nc.vector.memset(wb_raw_scales[:].bitcast(I32), 0)
+        load_scale_rows(nc, wb_raw_scales[:], wb_scales[0])
+        for j in range(2):
+            nc.vector.memset(f1[j][:], 0.0)
+
+        wa_dealt = tile([P, K], U32, "wa_dealt")
+        wa_plane = tile([P, K], U8, "wa_plane")
+        wb_dealt = tile([P, K], U16, "wb_dealt")
+        wb_plane = tile([P, K], U8, "wb_plane")
+        deal(nc, wa_dealt[:].bitcast(I32), wa_raw[:].bitcast(I32))
+
+        wb_raw = tile([P, K], U16, "wb_raw", tag="wa_raw")
+        nc.sync.dma_start(wb_raw[:].bitcast(I32), wb_words[0].bitcast(I32))
+
+        picked_words = [tile([P, HALF], U16, "picked_words%d" % h) for h in range(2)]
+        picked_scales = [tile([P, HALF], U8, "picked_scales%d" % h) for h in range(2)]
+        z_bank = [bank(j, "z_bank%d" % j) for j in range(PACK)]
+        z_sb = [tile([P, I], F32, "z_sb%d" % j) for j in range(PACK)]
+        c1 = [tile([P, U], F32, "c1_%d" % j) for j in range(PACK)]
+
+        def slots(h):
+            return slice(h * HALF, (h + 1) * HALF)
+
+        def pick_pages(h):
+            nc.vector.tensor_copy(picked_words[h][:], page_words[:].indirect(half_of(idx, h)))
+            nc.vector.tensor_copy(picked_scales[h][:], page_scales[:].indirect(half_of(idx, h)))
+
+        def z_product(j, h):
+            cols = slice(j * P, (j + 1) * P)
+            nc.tensor.matmul_mx(
+                z_bank[j][:, slots(h)],
+                lhsT=wa_dealt[:, cols].bitcast(FP8X4),
+                lhsT_scale=wa_plane[:, cols],
+                rhs=picked_words[h][:].bitcast(FP4X4),
+                rhs_scale=picked_scales[h][:],
+                start=True,
+                stop=True,
+            )
+
+        def h1_product(j, first_bank):
+            cols = slice(j * P, (j + 1) * P)
+            banks = []
+            for n in range(U // BANK):
+                notes = slice(n * BANK, (n + 1) * BANK)
+                acc = bank(first_bank + n, "h1_%d_%d" % (j, n))
+                nc.tensor.matmul_mx(
+                    acc[:],
+                    lhsT=wb_dealt[:, cols].bitcast(FP4X4),
+                    lhsT_scale=wb_plane[:, cols],
+                    rhs=note_words[:, notes].bitcast(FP8X4),
+                    rhs_scale=note_scales[:, notes],
+                    start=True,
+                    stop=True,
+                )
+                banks.append(acc)
+            return banks
+
+        def scalar_place(j, h):
+            nc.scalar.activation(f1[j][:].indirect(half_of(idx2, h)), z_sb[j][:, slots(h)], COPY)
+
+        def vector_place(j, h):
+            nc.vector.tensor_copy(f1[j][:].indirect(half_of(idx2, h)), z_sb[j][:, slots(h)])
+
+        def add_notes(j, banks):
+            for n, acc in enumerate(banks):
+                notes = slice(n * BANK, (n + 1) * BANK)
+                nc.vector.tensor_tensor(c1[j][:, notes], acc[:], f1[j][:, notes], ADD)
+
+        pick_pages(0)
+        deal(nc, wa_plane[:], wa_raw_scales[:])
+        f1.append(tile([P, U], F32, "f1_2", tag="wa_raw_scales"))
+        nc.gpsimd.memset(f1[2][:], 0.0)
+        for j in range(PACK):
+            z_product(j, 0)
+        pick_pages(1)
+        later_words = tile([P, U + E], U32, "later_words", tag="page_words")
+        note_words = later_words[:, 0:U]
+        wo_sb = later_words[:, U:]
+        nc.sync.dma_start(note_words.bitcast(I32), notes_words[0].rearrange("p n t -> p (n t)").bitcast(I32))
+        nc.sync.dma_start(wo_sb.bitcast(I32), wo_words[0].rearrange("p n t -> p (n t)").bitcast(I32))
+        later_planes = tile([P, U + E], U8, "later_planes", tag="page_scales")
+        note_scales = later_planes[:, 0:U]
+        wo_plane = later_planes[:, U:]
+        nc.gpsimd.memset(later_planes[:].bitcast(I32), 0)
+        load_scale_rows(nc, note_scales, notes_scales[0])
+        load_scale_rows(nc, wo_plane, wo_scales[0])
+        kf_sb = tile([P, PACK], F32, "kf_sb", tag="picked_words0")
+        nc.sync.dma_start(kf_sb[:], kf.rearrange("(p t) o -> p (t o)", t=PACK))
+        deal(nc, wb_plane[:], wb_raw_scales[:])
+        deal(nc, wb_dealt[:], wb_raw[:])
+        f1.append(tile([P, U], F32, "f1_3", tag="wa_raw"))
+        nc.gpsimd.memset(f1[3][:], 0.0)
+        nc.scalar.copy(z_sb[0][:, slots(0)], z_bank[0][:, slots(0)])
+        scalar_place(0, 0)
+        nc.vector.tensor_copy(z_sb[1][:, slots(0)], z_bank[1][:, slots(0)])
+        for j in (0, 2, 3, 1):
+            z_product(j, 1)
+        vector_place(1, 0)
+        h1 = [h1_product(0, 4), h1_product(1, 6)]
+        nc.scalar.copy(z_sb[0][:, slots(1)], z_bank[0][:, slots(1)])
+        scalar_place(0, 1)
+        nc.vector.tensor_copy(z_sb[1][:, slots(1)], z_bank[1][:, slots(1)])
+        vector_place(1, 1)
+        nc.scalar.copy(z_sb[2][:], z_bank[2][:])
+        scalar_place(2, 0)
+        h1.append(h1_product(2, 0))
+        add_notes(0, h1[0])
+        add_notes(1, h1[1])
+        scalar_place(2, 1)
+        nc.vector.tensor_copy(z_sb[3][:], z_bank[3][:])
+        h1.append(h1_product(3, 2))
+        vector_place(3, 0)
+        scalar_place(3, 1)
+        add_notes(2, h1[2])
+        add_notes(3, h1[3])
+
+        factor = kf_sb[:].rearrange("p (a t b) -> p a t b", a=1, b=1).to_broadcast([P, HALF // 4, PACK, 4])
+        out_rows = out.rearrange("(a p) i -> p a i", p=P)
+        looked = [tile([P, PACK, HALF], F32, "looked0"), tile([P, PACK, HALF], F32, "looked1", tag="wa_raw")]
+        for j in range(PACK):
+            nc.scalar.activation(looked[0][:, j, :], c1[j][:].indirect(half_of(idx3, 0)), COPY)
+        nc.vector.tensor_copy(looked[1][:, 0, :], c1[0][:].indirect(half_of(idx3, 1)))
+        for j in range(1, PACK):
+            nc.scalar.activation(looked[1][:, j, :], c1[j][:].indirect(half_of(idx3, 1)), COPY)
+        for h in range(2):
+            w16 = tile([P, HALF, PACK], BF16, "w16_%d" % h)
+            nc.vector.tensor_tensor(
+                w16[:].rearrange("p (c i) t -> p c t i", i=4),
+                looked[h][:].rearrange("p t (c i) -> p c t i", i=4),
+                factor,
+                MULT,
+            )
+            w_words = tile([P, HALF], U32, "w_words%d" % h)
+            w_plane = tile([P, HALF], U8, "w_plane%d" % h)
+            nc.vector.quantize_mx(w_words[:].bitcast(FP8X4), w_plane[:], w16[:].rearrange("p i t -> p (i t)"))
+            for a in range(E // P):
+                cols = slice(a * P, (a + 1) * P)
+                acc = bank(4 + 2 * h + a, "y_%d_%d" % (h, a))
+                nc.tensor.matmul_mx(
+                    acc[:, 0:HALF],
+                    lhsT=wo_sb[:, cols].bitcast(FP8X4),
+                    lhsT_scale=wo_plane[:, cols],
+                    rhs=w_words[:].bitcast(FP8X4),
+                    rhs_scale=w_plane[:],
+                    start=True,
+                    stop=True,
+                )
+                y_sb = tile([P, HALF], F32, "y_sb%d_%d" % (h, a))
+                if h == 1 and a == 1:
+                    nc.vector.tensor_copy(y_sb[:], acc[:, 0:HALF])
+                else:
+                    nc.scalar.copy(y_sb[:], acc[:, 0:HALF])
+                nc.sync.dma_start(out_rows[:, a, slots(h)], y_sb[:])

@@ -29,8 +29,8 @@ def load_scale_rows(nc, plane, rows):
         nc.sync.dma_start(plane[32 * q : 32 * q + 4, :].bitcast(I32), rows[4 * q : 4 * q + 4, :].bitcast(I32))
 
 
-def deal(nc, dealt, raw):
-    nc.vector.tensor_copy(dealt.rearrange("p (j m) -> p j m", j=PACK), raw.rearrange("p (m j) -> p j m", j=PACK))
+def deal(copy, dealt, raw, places=slice(0, PACK)):
+    copy(dealt.rearrange("p (j m) -> p j m", j=PACK)[:, places, :], raw.rearrange("p (m j) -> p j m", j=PACK)[:, places, :])
 
 
 def tile_attend_pagesintonotes_kernel(
@@ -80,7 +80,7 @@ def tile_attend_pagesintonotes_kernel(
         wa_plane = tile([P, K], U8, "wa_plane")
         wb_dealt = tile([P, K], U16, "wb_dealt")
         wb_plane = tile([P, K], U8, "wb_plane")
-        deal(nc, wa_dealt[:].bitcast(I32), wa_raw[:].bitcast(I32))
+        deal(nc.scalar.copy, wa_dealt[:], wa_raw[:])
 
         wb_raw = tile([P, K], U16, "wb_raw", tag="wa_raw")
         nc.sync.dma_start(wb_raw[:].bitcast(I32), wb_words[0].bitcast(I32))
@@ -88,7 +88,7 @@ def tile_attend_pagesintonotes_kernel(
         picked_words = [tile([P, HALF], U16, "picked_words%d" % h) for h in range(2)]
         picked_scales = [tile([P, HALF], U8, "picked_scales%d" % h) for h in range(2)]
         z_bank = [bank(j, "z_bank%d" % j) for j in range(PACK)]
-        z_sb = [tile([P, I], F32, "z_sb%d" % j) for j in range(PACK)]
+        z_sb = {j: tile([P, I], F32, "z_sb%d" % j) for j in (0, 2, 3)}
         c1 = [tile([P, U], F32, "c1_%d" % j) for j in range(PACK)]
 
         def slots(h):
@@ -131,8 +131,8 @@ def tile_attend_pagesintonotes_kernel(
         def scalar_place(j, h):
             nc.scalar.activation(f1[j][:].indirect(half_of(idx2, h)), z_sb[j][:, slots(h)], COPY)
 
-        def vector_place(j, h):
-            nc.vector.tensor_copy(f1[j][:].indirect(half_of(idx2, h)), z_sb[j][:, slots(h)])
+        def vector_place(j, h, values):
+            nc.vector.tensor_copy(f1[j][:].indirect(half_of(idx2, h)), values)
 
         def add_notes(j, banks):
             for n, acc in enumerate(banks):
@@ -140,13 +140,16 @@ def tile_attend_pagesintonotes_kernel(
                 nc.vector.tensor_tensor(c1[j][:, notes], acc[:], f1[j][:, notes], ADD)
 
         pick_pages(0)
-        deal(nc, wa_plane[:], wa_raw_scales[:])
+        deal(nc.vector.tensor_copy, wa_plane[:], wa_raw_scales[:], slice(0, 1))
+        deal(nc.vector.tensor_copy, wa_plane[:], wa_raw_scales[:], slice(1, PACK))
         f1.append(tile([P, U], F32, "f1_2", tag="wa_raw_scales"))
         nc.gpsimd.memset(f1[2][:], 0.0)
         for j in range(PACK):
             z_product(j, 0)
         pick_pages(1)
-        later_words = tile([P, U + E], U32, "later_words", tag="page_words")
+        f1.append(tile([P, U], F32, "f1_3", tag="page_words"))
+        nc.gpsimd.memset(f1[3][:], 0.0)
+        later_words = tile([P, U + E], U32, "later_words", tag="picked_words0")
         note_words = later_words[:, 0:U]
         wo_sb = later_words[:, U:]
         nc.sync.dma_start(note_words.bitcast(I32), notes_words[0].rearrange("p n t -> p (n t)").bitcast(I32))
@@ -157,23 +160,23 @@ def tile_attend_pagesintonotes_kernel(
         nc.gpsimd.memset(later_planes[:].bitcast(I32), 0)
         load_scale_rows(nc, note_scales, notes_scales[0])
         load_scale_rows(nc, wo_plane, wo_scales[0])
-        kf_sb = tile([P, PACK], F32, "kf_sb", tag="picked_words0")
+        kf_sb = tile([P, PACK], F32, "kf_sb", tag="picked_scales0")
         nc.sync.dma_start(kf_sb[:], kf.rearrange("(p t) o -> p (t o)", t=PACK))
-        deal(nc, wb_plane[:], wb_raw_scales[:])
-        deal(nc, wb_dealt[:], wb_raw[:])
-        f1.append(tile([P, U], F32, "f1_3", tag="wa_raw"))
-        nc.gpsimd.memset(f1[3][:], 0.0)
+        deal(nc.vector.tensor_copy, wb_plane[:], wb_raw_scales[:])
+        deal(nc.vector.tensor_copy, wb_dealt[:], wb_raw[:])
         nc.scalar.copy(z_sb[0][:, slots(0)], z_bank[0][:, slots(0)])
         scalar_place(0, 0)
-        nc.vector.tensor_copy(z_sb[1][:, slots(0)], z_bank[1][:, slots(0)])
+        z1_first = tile([P, HALF], F32, "z1_first")
+        nc.vector.tensor_copy(z1_first[:], z_bank[1][:, slots(0)])
         for j in (0, 2, 3, 1):
             z_product(j, 1)
-        vector_place(1, 0)
+        vector_place(1, 0, z1_first[:])
         h1 = [h1_product(0, 4), h1_product(1, 6)]
         nc.scalar.copy(z_sb[0][:, slots(1)], z_bank[0][:, slots(1)])
         scalar_place(0, 1)
-        nc.vector.tensor_copy(z_sb[1][:, slots(1)], z_bank[1][:, slots(1)])
-        vector_place(1, 1)
+        z1_second = tile([P, HALF], F32, "z1_second", tag="wa_raw")
+        nc.vector.tensor_copy(z1_second[:], z_bank[1][:, slots(1)])
+        vector_place(1, 1, z1_second[:])
         nc.scalar.copy(z_sb[2][:], z_bank[2][:])
         scalar_place(2, 0)
         h1.append(h1_product(2, 0))
@@ -182,35 +185,45 @@ def tile_attend_pagesintonotes_kernel(
         scalar_place(2, 1)
         nc.vector.tensor_copy(z_sb[3][:], z_bank[3][:])
         h1.append(h1_product(3, 2))
-        vector_place(3, 0)
+        vector_place(3, 0, z_sb[3][:, slots(0)])
         scalar_place(3, 1)
         add_notes(2, h1[2])
         add_notes(3, h1[3])
 
-        factor = kf_sb[:].rearrange("p (a t b) -> p a t b", a=1, b=1).to_broadcast([P, HALF // 4, PACK, 4])
         out_rows = out.rearrange("(a p) i -> p a i", p=P)
-        looked = [tile([P, PACK, HALF], F32, "looked0"), tile([P, PACK, HALF], F32, "looked1", tag="wa_raw")]
-        for j in range(PACK):
-            nc.scalar.activation(looked[0][:, j, :], c1[j][:].indirect(half_of(idx3, 0)), COPY)
-        nc.vector.tensor_copy(looked[1][:, 0, :], c1[0][:].indirect(half_of(idx3, 1)))
-        for j in range(1, PACK):
-            nc.scalar.activation(looked[1][:, j, :], c1[j][:].indirect(half_of(idx3, 1)), COPY)
-        for h in range(2):
-            w16 = tile([P, HALF, PACK], BF16, "w16_%d" % h)
+        looked = [tile([P, PACK, HALF], F32, "looked0"), tile([P, PACK, HALF], F32, "looked1", tag="page_words")]
+        pieces = [(0, HALF), (HALF, HALF + P), (HALF + P, I)]
+
+        def looked_up(j, first, last):
+            return looked[first // HALF][:, j, first % HALF : first % HALF + last - first]
+
+        def notes_of(j, first, last):
+            return c1[j][:].indirect(idx3[:, first // 16 : last // 16])
+
+        for n, (first, last) in enumerate(pieces):
+            if n == 1:
+                nc.vector.tensor_copy(looked_up(0, HALF, I), notes_of(0, HALF, I))
+            for j in range(0 if n == 0 else 1, PACK):
+                nc.scalar.activation(looked_up(j, first, last), notes_of(j, first, last), COPY)
+
+        for n, (first, last) in enumerate(pieces):
+            width = last - first
+            factor = kf_sb[:].rearrange("p (a t b) -> p a t b", a=1, b=1).to_broadcast([P, width // 4, PACK, 4])
+            w16 = tile([P, width, PACK], BF16, "w16_%d" % n)
             nc.vector.tensor_tensor(
                 w16[:].rearrange("p (c i) t -> p c t i", i=4),
-                looked[h][:].rearrange("p t (c i) -> p c t i", i=4),
+                looked_up(slice(0, PACK), first, last).rearrange("p t (c i) -> p c t i", i=4),
                 factor,
                 MULT,
             )
-            w_words = tile([P, HALF], U32, "w_words%d" % h)
-            w_plane = tile([P, HALF], U8, "w_plane%d" % h)
+            w_words = tile([P, width], U32, "w_words%d" % n)
+            w_plane = tile([P, width], U8, "w_plane%d" % n)
             nc.vector.quantize_mx(w_words[:].bitcast(FP8X4), w_plane[:], w16[:].rearrange("p i t -> p (i t)"))
+            acc = bank(4 + n, "y_%d" % n)
             for a in range(E // P):
                 cols = slice(a * P, (a + 1) * P)
-                acc = bank(4 + 2 * h + a, "y_%d_%d" % (h, a))
                 nc.tensor.matmul_mx(
-                    acc[:, 0:HALF],
+                    acc[:, a * width : (a + 1) * width],
                     lhsT=wo_sb[:, cols].bitcast(FP8X4),
                     lhsT_scale=wo_plane[:, cols],
                     rhs=w_words[:].bitcast(FP8X4),
@@ -218,9 +231,6 @@ def tile_attend_pagesintonotes_kernel(
                     start=True,
                     stop=True,
                 )
-                y_sb = tile([P, HALF], F32, "y_sb%d_%d" % (h, a))
-                if h == 1 and a == 1:
-                    nc.vector.tensor_copy(y_sb[:], acc[:, 0:HALF])
-                else:
-                    nc.scalar.copy(y_sb[:], acc[:, 0:HALF])
-                nc.sync.dma_start(out_rows[:, a, slots(h)], y_sb[:])
+            y_sb = tile([P, 2 * width], F32, "y_sb%d" % n)
+            nc.scalar.copy(y_sb[:], acc[:, 0 : 2 * width])
+            nc.sync.dma_start(out_rows[:, :, first:last], y_sb[:].rearrange("p (a i) -> p a i", a=E // P))

from contextlib import ExitStack

import concourse.mybir as mybir

D, K, T, U, I, E = 512, 512, 2048, 1024, 512, 256
FLOPS = 2 * (D * K * I + D * K * U + K * E * I)

F32 = mybir.dt.float32
BF16 = mybir.dt.bfloat16
I32 = mybir.dt.int32
U32 = mybir.dt.uint32
U16 = mybir.dt.uint16
U8 = mybir.dt.uint8
FP8X4 = mybir.dt.float8_e4m3fn_x4
FP4X4 = mybir.dt.float4_e2m1fn_x4
COPY = mybir.ActivationFunctionType.Copy
ADD = mybir.AluOpType.add
MULT = mybir.AluOpType.mult

P = 128
PACK = 4
BANK = 512
HALF = I // 2
LIST_COLS = I // 16


def load_scale_rows(nc, plane, rows):
    for q in range(4):
        nc.sync.dma_start(plane[32 * q : 32 * q + 4, :].bitcast(I32), rows[4 * q : 4 * q + 4, :].bitcast(I32))


def deal(copy, dealt, raw, places=slice(0, PACK)):
    copy(dealt.rearrange("p (j m) -> p j m", j=PACK)[:, places, :], raw.rearrange("p (m j) -> p j m", j=PACK)[:, places, :])


def tile_attend_pagesintonotes_kernel(
    tc, pages_words, pages_scales, wa_words, wa_scales, notes_words, notes_scales, wb_words, wb_scales, kf, wo_words, wo_scales, offs, offs2, offs3, out
):
    nc = tc.nc
    with ExitStack() as ctx:
        sb = ctx.enter_context(tc.tile_pool(name="sb", bufs=1))
        psum = ctx.enter_context(tc.psum_pool(name="psum", bufs=1))

        def tile(shape, dtype, name, tag=None):
            return sb.tile(shape, dtype, name=name, tag=tag or name, align_bytes=64)

        def bank(b, name):
            return psum.tile([P, BANK], F32, name=name, tag="bank%d" % b)

        def half_of(lst, h):
            return lst[:, h * LIST_COLS // 2 : (h + 1) * LIST_COLS // 2]

        idx = tile([P, LIST_COLS], U16, "idx")
        idx2 = tile([P, LIST_COLS], U16, "idx2")
        idx3 = tile([P, LIST_COLS], U16, "idx3")
        page_words = tile([P, T], U16, "page_words")
        page_scales = tile([P, T], U8, "page_scales")
        wa_raw = tile([P, K], U32, "wa_raw")
        wa_raw_scales = tile([P, K], U8, "wa_raw_scales")
        wb_raw_scales = tile([P, K], U8, "wb_raw_scales")
        f1 = [tile([P, U], F32, "f1_%d" % j) for j in range(2)]

        nc.vector.memset(page_scales[:].bitcast(I32), 0)
        nc.vector.memset(wa_raw_scales[:].bitcast(I32), 0)

        nc.sync.dma_start(idx[:], offs)
        nc.sync.dma_start(page_words[:].bitcast(I32), pages_words[0].bitcast(I32))
        nc.sync.dma_start(wa_raw[:].bitcast(I32), wa_words[0].rearrange("p n t -> p (n t)").bitcast(I32))
        load_scale_rows(nc, page_scales[:], pages_scales[0])
        load_scale_rows(nc, wa_raw_scales[:], wa_scales[0])
        nc.sync.dma_start(idx2[:], offs2)
        nc.sync.dma_start(idx3[:], offs3)

        nc.vector.memset(wb_raw_scales[:].bitcast(I32), 0)
        load_scale_rows(nc, wb_raw_scales[:], wb_scales[0])
        for j in range(2):
            nc.vector.memset(f1[j][:], 0.0)

        wa_dealt = tile([P, K], U32, "wa_dealt")
        wa_plane = tile([P, K], U8, "wa_plane")
        wb_dealt = tile([P, K], U16, "wb_dealt")
        wb_plane = tile([P, K], U8, "wb_plane")
        deal(nc.scalar.copy, wa_dealt[:], wa_raw[:])

        wb_raw = tile([P, K], U16, "wb_raw", tag="wa_raw")
        nc.sync.dma_start(wb_raw[:].bitcast(I32), wb_words[0].bitcast(I32))

        picked_words = [tile([P, HALF], U16, "picked_words%d" % h) for h in range(2)]
        picked_scales = [tile([P, HALF], U8, "picked_scales%d" % h) for h in range(2)]
        z_bank = [bank(j, "z_bank%d" % j) for j in range(PACK)]
        z_sb = {j: tile([P, I], F32, "z_sb%d" % j) for j in (0, 2, 3)}
        c1 = [tile([P, U], F32, "c1_%d" % j) for j in range(PACK)]

        def slots(h):
            return slice(h * HALF, (h + 1) * HALF)

        def pick_pages(h):
            nc.vector.tensor_copy(picked_words[h][:], page_words[:].indirect(half_of(idx, h)))
            nc.vector.tensor_copy(picked_scales[h][:], page_scales[:].indirect(half_of(idx, h)))

        def z_product(j, h):
            cols = slice(j * P, (j + 1) * P)
            nc.tensor.matmul_mx(
                z_bank[j][:, slots(h)],
                lhsT=wa_dealt[:, cols].bitcast(FP8X4),
                lhsT_scale=wa_plane[:, cols],
                rhs=picked_words[h][:].bitcast(FP4X4),
                rhs_scale=picked_scales[h][:],
                start=True,
                stop=True,
            )

        def h1_product(j, first_bank):
            cols = slice(j * P, (j + 1) * P)
            banks = []
            for n in range(U // BANK):
                notes = slice(n * BANK, (n + 1) * BANK)
                acc = bank(first_bank + n, "h1_%d_%d" % (j, n))
                nc.tensor.matmul_mx(
                    acc[:],
                    lhsT=wb_dealt[:, cols].bitcast(FP4X4),
                    lhsT_scale=wb_plane[:, cols],
                    rhs=note_words[:, notes].bitcast(FP8X4),
                    rhs_scale=note_scales[:, notes],
                    start=True,
                    stop=True,
                )
                banks.append(acc)
            return banks

        def scalar_place(j, h):
            nc.scalar.activation(f1[j][:].indirect(half_of(idx2, h)), z_sb[j][:, slots(h)], COPY)

        def vector_place(j, h, values):
            nc.vector.tensor_copy(f1[j][:].indirect(half_of(idx2, h)), values)

        def add_notes(j, banks):
            for n, acc in enumerate(banks):
                notes = slice(n * BANK, (n + 1) * BANK)
                nc.vector.tensor_tensor(c1[j][:, notes], acc[:], f1[j][:, notes], ADD)

        pick_pages(0)
        deal(nc.vector.tensor_copy, wa_plane[:], wa_raw_scales[:], slice(0, 1))
        deal(nc.vector.tensor_copy, wa_plane[:], wa_raw_scales[:], slice(1, PACK))
        f1.append(tile([P, U], F32, "f1_2", tag="wa_raw_scales"))
        nc.gpsimd.memset(f1[2][:], 0.0)
        for j in range(PACK):
            z_product(j, 0)
        pick_pages(1)
        f1.append(tile([P, U], F32, "f1_3", tag="page_words"))
        nc.gpsimd.memset(f1[3][:], 0.0)
        later_words = tile([P, U + E], U32, "later_words", tag="picked_words0")
        note_words = later_words[:, 0:U]
        wo_sb = later_words[:, U:]
        nc.sync.dma_start(note_words.bitcast(I32), notes_words[0].rearrange("p n t -> p (n t)").bitcast(I32))
        nc.sync.dma_start(wo_sb.bitcast(I32), wo_words[0].rearrange("p n t -> p (n t)").bitcast(I32))
        later_planes = tile([P, U + E], U8, "later_planes", tag="page_scales")
        note_scales = later_planes[:, 0:U]
        wo_plane = later_planes[:, U:]
        nc.gpsimd.memset(later_planes[:].bitcast(I32), 0)
        load_scale_rows(nc, note_scales, notes_scales[0])
        load_scale_rows(nc, wo_plane, wo_scales[0])
        kf_sb = tile([P, PACK], F32, "kf_sb", tag="picked_scales0")
        nc.sync.dma_start(kf_sb[:], kf.rearrange("(p t) o -> p (t o)", t=PACK))
        deal(nc.vector.tensor_copy, wb_plane[:], wb_raw_scales[:])
        deal(nc.vector.tensor_copy, wb_dealt[:], wb_raw[:])
        nc.scalar.copy(z_sb[0][:, slots(0)], z_bank[0][:, slots(0)])
        scalar_place(0, 0)
        z1_first = tile([P, HALF], F32, "z1_first")
        nc.vector.tensor_copy(z1_first[:], z_bank[1][:, slots(0)])
        for j in (0, 2, 3, 1):
            z_product(j, 1)
        vector_place(1, 0, z1_first[:])
        h1 = [h1_product(0, 4), h1_product(1, 6)]
        nc.scalar.copy(z_sb[0][:, slots(1)], z_bank[0][:, slots(1)])
        scalar_place(0, 1)
        z1_second = tile([P, HALF], F32, "z1_second", tag="wa_raw")
        nc.vector.tensor_copy(z1_second[:], z_bank[1][:, slots(1)])
        vector_place(1, 1, z1_second[:])
        nc.scalar.copy(z_sb[2][:], z_bank[2][:])
        scalar_place(2, 0)
        h1.append(h1_product(2, 0))
        add_notes(0, h1[0])
        add_notes(1, h1[1])
        scalar_place(2, 1)
        nc.vector.tensor_copy(z_sb[3][:], z_bank[3][:])
        h1.append(h1_product(3, 2))
        vector_place(3, 0, z_sb[3][:, slots(0)])
        scalar_place(3, 1)
        add_notes(2, h1[2])
        add_notes(3, h1[3])

        out_rows = out.rearrange("(a p) i -> p a i", p=P)
        looked = [tile([P, PACK, HALF], F32, "looked0"), tile([P, PACK, HALF], F32, "looked1", tag="page_words")]
        pieces = [(0, HALF), (HALF, HALF + P), (HALF + P, I)]

        def looked_up(j, first, last):
            return looked[first // HALF][:, j, first % HALF : first % HALF + last - first]

        def notes_of(j, first, last):
            return c1[j][:].indirect(idx3[:, first // 16 : last // 16])

        for n, (first, last) in enumerate(pieces):
            if n == 1:
                nc.vector.tensor_copy(looked_up(0, HALF, I), notes_of(0, HALF, I))
            for j in range(0 if n == 0 else 1, PACK):
                nc.scalar.activation(looked_up(j, first, last), notes_of(j, first, last), COPY)

        for n, (first, last) in enumerate(pieces):
            width = last - first
            factor = kf_sb[:].rearrange("p (a t b) -> p a t b", a=1, b=1).to_broadcast([P, width // 4, PACK, 4])
            w16 = tile([P, width, PACK], BF16, "w16_%d" % n)
            nc.vector.tensor_tensor(
                w16[:].rearrange("p (c i) t -> p c t i", i=4),
                looked_up(slice(0, PACK), first, last).rearrange("p t (c i) -> p c t i", i=4),
                factor,
                MULT,
            )
            w_words = tile([P, width], U32, "w_words%d" % n)
            w_plane = tile([P, width], U8, "w_plane%d" % n)
            nc.vector.quantize_mx(w_words[:].bitcast(FP8X4), w_plane[:], w16[:].rearrange("p i t -> p (i t)"))
            acc = bank(4 + n, "y_%d" % n)
            for a in range(E // P):
                cols = slice(a * P, (a + 1) * P)
                nc.tensor.matmul_mx(
                    acc[:, a * width : (a + 1) * width],
                    lhsT=wo_sb[:, cols].bitcast(FP8X4),
                    lhsT_scale=wo_plane[:, cols],
                    rhs=w_words[:].bitcast(FP8X4),
                    rhs_scale=w_plane[:],
                    start=True,
                    stop=True,
                )
            y_sb = tile([P, 2 * width], F32, "y_sb%d" % n)
            nc.scalar.copy(y_sb[:], acc[:, 0 : 2 * width])
            nc.sync.dma_start(out_rows[:, :, first:last], y_sb[:].rearrange("p (a i) -> p a i", a=E // P))
